import numpy as np
import ml_dtypes

BF16 = ml_dtypes.bfloat16


def bf(x):
    return np.asarray(x, np.float32).astype(BF16)


def f32(x):
    return np.asarray(x, np.float32)


def f64(x):
    return np.asarray(x).astype(np.float64)


def striped(idx):
    return np.tile(idx.reshape(-1, 16).T, (8, 1))


def rows(idx, k):
    return np.tile(idx, (k, 1))


def look(tab, idx):
    return np.take_along_axis(f64(tab), rows(idx, len(tab)), axis=1)


K, S, V, N = 256, 2048, 512, 512


def silu(v):
    return v / (1.0 + np.exp(-v))


def setup_inputs():
    return {"tab": f32(np.random.standard_normal((2, K, S))), "y": f32(np.random.standard_normal((K, V))), "offs": striped(np.random.permutation(S)[:N])}


def reference(tab, y, offs):
    idx = offs[:16].T.reshape(-1)
    x = (look(tab[0], idx) * f64(y)) * (silu(look(tab[1], idx)))
    return x

@@ -1,0 +1,35 @@
+import concourse.mybir as mybir
+
+P = 128
+F32 = mybir.dt.float32
+U16 = mybir.dt.uint16
+MULT = mybir.AluOpType.mult
+SILU = mybir.ActivationFunctionType.Silu
+
+
+def tile_lookup_vg_mulsilu_out_kernel(tc, tab, y, offs, out):
+    nc = tc.nc
+    rows, places = tab.shape[1], tab.shape[2]
+    entries = y.shape[1]
+    blocks = rows // P
+
+    with tc.tile_pool(name="held", bufs=1) as held, tc.tile_pool(name="work", bufs=blocks) as work:
+        offsets = held.tile([P, entries // 16], U16, name="offsets")
+        nc.sync.dma_start(offsets[:], offs)
+
+        for block in range(blocks):
+            block_rows = slice(block * P, (block + 1) * P)
+            gates = work.tile([P, places], F32, name="gates")
+            values = work.tile([P, places], F32, name="values")
+            stream = work.tile([P, entries], F32, name="stream")
+            nc.sync.dma_start(gates[:], tab[1, block_rows, :])
+            nc.sync.dma_start(stream[:], y[block_rows, :])
+            nc.sync.dma_start(values[:], tab[0, block_rows, :])
+
+            gated = work.tile([P, entries], F32, name="gated")
+            scaled = work.tile([P, entries], F32, name="scaled")
+            result = work.tile([P, entries], F32, name="result")
+            nc.scalar.activation(gated[:], gates[:].indirect(offsets[:]), SILU)
+            nc.vector.tensor_tensor(scaled[:], values[:].indirect(offsets[:]), stream[:], MULT)
+            nc.vector.tensor_tensor(result[:], scaled[:], gated[:], MULT)
+            nc.sync.dma_start(out[block_rows, :], result[:])

@@ -5,6 +5,8 @@ F32 = mybir.dt.float32
 U16 = mybir.dt.uint16
 MULT = mybir.AluOpType.mult
 SILU = mybir.ActivationFunctionType.Silu
+PER_COLUMN = 16
+PIECE = 128
 
 
 def tile_lookup_vg_mulsilu_out_kernel(tc, tab, y, offs, out):
@@ -14,22 +16,29 @@ def tile_lookup_vg_mulsilu_out_kernel(tc, tab, y, offs, out):
     blocks = rows // P
 
     with tc.tile_pool(name="held", bufs=1) as held, tc.tile_pool(name="work", bufs=blocks) as work:
-        offsets = held.tile([P, entries // 16], U16, name="offsets")
+        offsets = held.tile([P, entries // PER_COLUMN], U16, name="offsets")
         nc.sync.dma_start(offsets[:], offs)
+
+        gates, stream, values = [], [], []
+        for block in range(blocks):
+            block_rows = slice(block * P, (block + 1) * P)
+            gates.append(work.tile([P, places], F32, name="gates"))
+            stream.append(work.tile([P, entries], F32, name="stream"))
+            values.append(work.tile([P, places], F32, name="values"))
+            nc.sync.dma_start(gates[block][:], tab[1, block_rows, :])
+            nc.sync.dma_start(stream[block][:], y[block_rows, :])
+            nc.sync.dma_start(values[block][:], tab[0, block_rows, :])
 
         for block in range(blocks):
             block_rows = slice(block * P, (block + 1) * P)
-            gates = work.tile([P, places], F32, name="gates")
-            values = work.tile([P, places], F32, name="values")
-            stream = work.tile([P, entries], F32, name="stream")
-            nc.sync.dma_start(gates[:], tab[1, block_rows, :])
-            nc.sync.dma_start(stream[:], y[block_rows, :])
-            nc.sync.dma_start(values[:], tab[0, block_rows, :])
-
+            silu = work.tile([P, entries], F32, name="silu")
             gated = work.tile([P, entries], F32, name="gated")
-            scaled = work.tile([P, entries], F32, name="scaled")
             result = work.tile([P, entries], F32, name="result")
-            nc.scalar.activation(gated[:], gates[:].indirect(offsets[:]), SILU)
-            nc.vector.tensor_tensor(scaled[:], values[:].indirect(offsets[:]), stream[:], MULT)
-            nc.vector.tensor_tensor(result[:], scaled[:], gated[:], MULT)
-            nc.sync.dma_start(out[block_rows, :], result[:])
+            nc.scalar.activation(silu[:], gates[block][:].indirect(offsets[:]), SILU)
+            nc.vector.tensor_tensor(gated[:], stream[block][:], silu[:], MULT)
+            for first in range(0, entries, PIECE):
+                piece = slice(first, first + PIECE)
+                piece_offsets = offsets[:, first // PER_COLUMN : (first + PIECE) // PER_COLUMN]
+                looked_up = values[block][:].indirect(piece_offsets)
+                nc.vector.tensor_tensor(result[:, piece], looked_up, gated[:, piece], MULT)
+                nc.sync.dma_start(out[block_rows, piece], result[:, piece])

@@ -14,31 +14,35 @@ def tile_lookup_vg_mulsilu_out_kernel(tc, tab, y, offs, out):
     rows, places = tab.shape[1], tab.shape[2]
     entries = y.shape[1]
     blocks = rows // P
+    tab_blocks = tab.rearrange("t (p b) s -> t b p s", b=blocks)
+    out_blocks = out.rearrange("(p b) n -> b p n", b=blocks)
 
     with tc.tile_pool(name="held", bufs=1) as held, tc.tile_pool(name="work", bufs=blocks) as work:
         offsets = held.tile([P, entries // PER_COLUMN], U16, name="offsets")
+        stream = held.tile([P, blocks, entries], F32, name="stream")
+        gates = [work.tile([P, places], F32, name="gates") for block in range(blocks)]
+        values = [work.tile([P, places], F32, name="values") for block in range(blocks)]
+
+        nc.sync.dma_start(gates[0][:], tab_blocks[1, 0])
         nc.sync.dma_start(offsets[:], offs)
-
-        gates, stream, values = [], [], []
+        nc.sync.dma_start(stream[:], y.rearrange("(p b) n -> p b n", b=blocks))
+        for block in range(1, blocks):
+            nc.sync.dma_start(gates[block][:], tab_blocks[1, block])
         for block in range(blocks):
-            block_rows = slice(block * P, (block + 1) * P)
-            gates.append(work.tile([P, places], F32, name="gates"))
-            stream.append(work.tile([P, entries], F32, name="stream"))
-            values.append(work.tile([P, places], F32, name="values"))
-            nc.sync.dma_start(gates[block][:], tab[1, block_rows, :])
-            nc.sync.dma_start(stream[block][:], y[block_rows, :])
-            nc.sync.dma_start(values[block][:], tab[0, block_rows, :])
+            nc.sync.dma_start(values[block][:], tab_blocks[0, block])
 
+        gated = []
         for block in range(blocks):
-            block_rows = slice(block * P, (block + 1) * P)
             silu = work.tile([P, entries], F32, name="silu")
-            gated = work.tile([P, entries], F32, name="gated")
-            result = work.tile([P, entries], F32, name="result")
+            gated.append(work.tile([P, entries], F32, name="gated"))
             nc.scalar.activation(silu[:], gates[block][:].indirect(offsets[:]), SILU)
-            nc.vector.tensor_tensor(gated[:], stream[block][:], silu[:], MULT)
+            nc.vector.tensor_tensor(gated[block][:], stream[:, block, :], silu[:], MULT)
+
+        for block in range(blocks):
+            result = work.tile([P, entries], F32, name="result")
             for first in range(0, entries, PIECE):
                 piece = slice(first, first + PIECE)
                 piece_offsets = offsets[:, first // PER_COLUMN : (first + PIECE) // PER_COLUMN]
                 looked_up = values[block][:].indirect(piece_offsets)
-                nc.vector.tensor_tensor(result[:, piece], looked_up, gated[:, piece], MULT)
-                nc.sync.dma_start(out[block_rows, piece], result[:, piece])
+                nc.vector.tensor_tensor(result[:, piece], looked_up, gated[block][:, piece], MULT)
+                nc.sync.dma_start(out_blocks[block, :, piece], result[:, piece])

import concourse.mybir as mybir

P = 128
F32 = mybir.dt.float32
U16 = mybir.dt.uint16
MULT = mybir.AluOpType.mult
SILU = mybir.ActivationFunctionType.Silu
PER_COLUMN = 16
PIECE = 128


def tile_lookup_vg_mulsilu_out_kernel(tc, tab, y, offs, out):
    nc = tc.nc
    rows, places = tab.shape[1], tab.shape[2]
    entries = y.shape[1]
    blocks = rows // P
    tab_blocks = tab.rearrange("t (p b) s -> t b p s", b=blocks)
    out_blocks = out.rearrange("(p b) n -> b p n", b=blocks)

    with tc.tile_pool(name="held", bufs=1) as held, tc.tile_pool(name="work", bufs=blocks) as work:
        offsets = held.tile([P, entries // PER_COLUMN], U16, name="offsets")
        stream = held.tile([P, blocks, entries], F32, name="stream")
        gates = [work.tile([P, places], F32, name="gates") for block in range(blocks)]
        values = [work.tile([P, places], F32, name="values") for block in range(blocks)]

        nc.sync.dma_start(gates[0][:], tab_blocks[1, 0])
        nc.sync.dma_start(offsets[:], offs)
        nc.sync.dma_start(stream[:], y.rearrange("(p b) n -> p b n", b=blocks))
        for block in range(1, blocks):
            nc.sync.dma_start(gates[block][:], tab_blocks[1, block])
        for block in range(blocks):
            nc.sync.dma_start(values[block][:], tab_blocks[0, block])

        gated = []
        for block in range(blocks):
            silu = work.tile([P, entries], F32, name="silu")
            gated.append(work.tile([P, entries], F32, name="gated"))
            nc.scalar.activation(silu[:], gates[block][:].indirect(offsets[:]), SILU)
            nc.vector.tensor_tensor(gated[block][:], stream[:, block, :], silu[:], MULT)

        for block in range(blocks):
            result = work.tile([P, entries], F32, name="result")
            for first in range(0, entries, PIECE):
                piece = slice(first, first + PIECE)
                piece_offsets = offsets[:, first // PER_COLUMN : (first + PIECE) // PER_COLUMN]
                looked_up = values[block][:].indirect(piece_offsets)
                nc.vector.tensor_tensor(result[:, piece], looked_up, gated[block][:, piece], MULT)
                nc.sync.dma_start(out_blocks[block, :, piece], result[:, piece])
